import numpy as np
import ml_dtypes


def mxq(x, axis, fmt="e4m3"):
    dtype, down = {"e4m3": (ml_dtypes.float8_e4m3fn, 7), "e5m2": (ml_dtypes.float8_e5m2, 14)}[fmt]
    v = np.moveaxis(np.asarray(x, np.float32).astype(ml_dtypes.bfloat16).astype(np.float64), axis, -1)
    blocks = v.reshape(v.shape[:-1] + (-1, 32))
    amax = np.abs(blocks).max(-1, keepdims=True)
    byte = np.maximum(np.where(amax > 0, np.frexp(amax)[1] - 1 + 127, 0) - down, 1)
    scale = np.exp2(byte - 127.0)
    codes = (blocks / scale).astype(np.float32).astype(dtype).astype(np.float64)
    return np.moveaxis((codes * scale).reshape(v.shape), -1, axis)


WIDE = False


def mx_kscale(k):
    if not WIDE:
        return np.ones(k)
    levels = np.array([30, -30])
    if k % 512:
        return np.exp2(np.random.permutation(np.resize(levels, k // 32))).repeat(32)
    a = np.empty((k // 512, 16))
    for p in range(k // 512):
        a[p, :8] = np.random.permutation(np.resize(levels, 8))
        for g in range(8):
            far = levels[np.abs(levels - a[p, g]) >= 10]
            a[p, g + 8] = far[np.random.randint(len(far))]
    return np.exp2(a.ravel()).repeat(32)


def f64(x):
    return np.asarray(x).astype(np.float64)


def striped(idx):
    return np.tile(np.asarray(idx).reshape(-1, 16).T, (8, 1)).astype(np.uint16)


def unstriped(offs):
    return offs[:16].T.reshape(-1).astype(np.int64)


E2M1 = np.array([0.0, 0.5, 1.0, 1.5, 2.0, 3.0, 4.0, 6.0, -0.0, -0.5, -1.0, -1.5, -2.0, -3.0, -4.0, -6.0])


def pack_weight(w, fmt):
    k, n = w.shape
    w = f64(np.asarray(w, np.float32).astype(ml_dtypes.bfloat16)).reshape(k // 32, 32, n)
    amax = np.abs(w).max(1)
    if fmt in ("e4m3", "e5m2"):
        byte = np.frexp(amax)[1] - 1 + 127 - (7 if fmt == "e4m3" else 14)
    else:
        mant, ex = np.frexp(amax / 6.0)
        byte = np.where(mant > 0.5, ex, ex - 1) + 127
    byte = np.clip(np.where(amax > 0, byte, 1), 1, 254)
    scaled = (w * np.exp2(127.0 - byte)[:, None, :]).reshape(k, n).astype(np.float32)
    by_word = np.ascontiguousarray(scaled.reshape(k // 512, 128, 4, n).transpose(0, 1, 3, 2))
    if fmt in ("e4m3", "e5m2"):
        words = by_word.astype(ml_dtypes.float8_e4m3fn if fmt == "e4m3" else ml_dtypes.float8_e5m2).view(np.uint8)
    else:
        c = by_word.astype(ml_dtypes.float4_e2m1fn).view(np.uint8) & 0xF
        words = (c[..., 0::2] | (c[..., 1::2] << 4)).reshape(k // 512, 128, 2 * n)
    return np.ascontiguousarray(words), np.ascontiguousarray(byte.astype(np.uint8).reshape(k // 512, 16, n))


def unpack_weight(words, scales, fmt):
    g, _, n = scales.shape
    words = np.ascontiguousarray(words).reshape(g, 128, n, -1)
    if fmt in ("e4m3", "e5m2"):
        vals = words.view(ml_dtypes.float8_e4m3fn if fmt == "e4m3" else ml_dtypes.float8_e5m2).astype(np.float64)
    else:
        nib = np.empty((g, 128, n, 4), np.uint8)
        nib[..., 0::2] = words & 0xF
        nib[..., 1::2] = words >> 4
        vals = E2M1[nib]
    vals = vals * np.repeat(np.exp2(scales.astype(np.float64) - 127.0), 8, axis=1)[..., None]
    return vals.transpose(0, 1, 3, 2).reshape(g * 512, n)


K, T, Z, J, R, C, O, N, L, E = 512, 1024, 1024, 256, 512, 512, 256, 256, 512, 128


def setup_inputs():
    n = np.random.standard_normal
    idx = np.random.permutation(T)[:J]
    idx2 = np.random.permutation(Z)[:J]
    idx3 = np.random.permutation(C)[:J]
    idx4 = np.random.permutation(C)[:J]
    idx5 = np.random.permutation(C)[:O]
    idx6 = np.random.permutation(O)[:E]
    idx7 = np.random.permutation(O)[:E]
    fk = mx_kscale(K)
    fr = mx_kscale(R)
    fl = mx_kscale(L)
    xtp = pack_weight(n((K, T)) / fk[:, None], "e5m2")
    xop = pack_weight(n((K, Z)) / fk[:, None], "e4m3")
    wp = pack_weight(n((K, R)) * 1 / np.sqrt(K) * fk[:, None] * fr, "e2m1")
    wbp = pack_weight(n((R, N)) * 1 / np.sqrt(R) / fr[:, None], "e2m1")
    sxp = pack_weight(n((L, O)) / fl[:, None], "e4m3")
    wsp = pack_weight(n((L, N)) * 1 / np.sqrt(L) * fl[:, None], "e2m1")
    return {
        "xt_words": xtp[0],
        "xt_scales": xtp[1],
        "xo_words": xop[0],
        "xo_scales": xop[1],
        "w_words": wp[0],
        "w_scales": wp[1],
        "wb_words": wbp[0],
        "wb_scales": wbp[1],
        "sx_words": sxp[0],
        "sx_scales": sxp[1],
        "ws_words": wsp[0],
        "ws_scales": wsp[1],
        "offs": striped(idx),
        "offs2": striped(idx2),
        "offs3": striped(idx3),
        "offs4": striped(idx4),
        "offs5": striped(idx5),
        "offs6": striped(idx6),
        "offs7": striped(idx7),
    }


def reference(xt_words, xt_scales, xo_words, xo_scales, w_words, w_scales, wb_words, wb_scales, sx_words, sx_scales, ws_words, ws_scales, offs, offs2, offs3, offs4, offs5, offs6, offs7):
    idx = unstriped(offs)
    idx2 = unstriped(offs2)
    idx3 = unstriped(offs3)
    idx4 = unstriped(offs4)
    idx5 = unstriped(offs5)
    idx6 = unstriped(offs6)
    idx7 = unstriped(offs7)
    xtu = unpack_weight(xt_words, xt_scales, "e5m2")
    xou = unpack_weight(xo_words, xo_scales, "e4m3")
    wu = unpack_weight(w_words, w_scales, "e2m1")
    wbu = unpack_weight(wb_words, wb_scales, "e2m1")
    sxu = unpack_weight(sx_words, sx_scales, "e4m3")
    wsu = unpack_weight(ws_words, ws_scales, "e2m1")
    xtidxg = xtu[:, idx]
    a = wu.T @ xtidxg
    xoidx2g = xou[:, idx2]
    b = wu.T @ xoidx2g
    pw = np.zeros((R, C))
    pw[:, idx3] = a
    pv = np.zeros((R, C))
    pv[:, idx4] = b
    pg = pw + pv
    hid = pg[:, idx5]
    hidq = mxq(hid, 0, "e4m3")
    p = wbu.T @ hidq + wsu.T @ sxu
    y = np.maximum(p[:, idx6], p[:, idx7])
    return y

@@ -1,0 +1,206 @@
+from contextlib import ExitStack
+
+import concourse.mybir as mybir
+
+K, T, Z, J, R, C, O, N, L, E = 512, 1024, 1024, 256, 512, 512, 256, 256, 512, 128
+FLOPS = 2 * (2 * K * R * J + R * N * O + L * N * O)
+
+F32 = mybir.dt.float32
+BF16 = mybir.dt.bfloat16
+I32 = mybir.dt.int32
+U32 = mybir.dt.uint32
+U16 = mybir.dt.uint16
+U8 = mybir.dt.uint8
+E4M3 = mybir.dt.float8_e4m3fn_x4
+E5M2 = mybir.dt.float8_e5m2_x4
+E2M1 = mybir.dt.float4_e2m1fn_x4
+COPY = mybir.ActivationFunctionType.Copy
+ADD = mybir.AluOpType.add
+MAX = mybir.AluOpType.max
+
+P = 128
+PACK = 4
+
+
+def tile_list_oneforboth_shared_skip_bestoftwo_kernel(
+    tc, xt_words, xt_scales, xo_words, xo_scales, w_words, w_scales, wb_words, wb_scales,
+    sx_words, sx_scales, ws_words, ws_scales, offs, offs2, offs3, offs4, offs5, offs6, offs7, out,
+):
+    nc = tc.nc
+    with ExitStack() as ctx:
+        sb = ctx.enter_context(tc.tile_pool(name="sb", bufs=1))
+        ps = ctx.enter_context(tc.psum_pool(name="ps", bufs=1))
+
+        def tile(name, cols, dtype, tag=None):
+            return sb.tile([P, cols], dtype, name=name, tag=tag or name, align_bytes=64)
+
+        def load_list(name, src):
+            t = sb.tile([P, src.shape[1]], U16, name=name)
+            nc.sync.dma_start(t[:], src)
+            return t
+
+        def load_words8(name, src):
+            t = tile(name, src.shape[2], U32)
+            nc.sync.dma_start(t[:].bitcast(I32), src[0].rearrange("p n t -> p (n t)").bitcast(I32))
+            return t
+
+        def load_words4(name, src):
+            t = tile(name, src.shape[2], U8)
+            nc.sync.dma_start(t[:].bitcast(I32), src[0].bitcast(I32))
+            return t
+
+        def plane(name, src):
+            t = tile(name, src.shape[2], U8)
+            nc.vector.memset(t[:].bitcast(I32), 0)
+            return t
+
+        def load_plane(t, src):
+            for q in range(4):
+                nc.sync.dma_start(t[32 * q : 32 * q + 4, :].bitcast(I32), src[0, 4 * q : 4 * q + 4, :].bitcast(I32))
+
+        xt_s = plane("xt_s", xt_scales)
+        w_s = plane("w_s", w_scales)
+        xo_s = plane("xo_s", xo_scales)
+        wb_s = plane("wb_s", wb_scales)
+        ws_s = plane("ws_s", ws_scales)
+        sx_s = plane("sx_s", sx_scales)
+
+        l1 = load_list("l1", offs)
+        w_w = load_words4("w_w", w_words)
+        load_plane(xt_s, xt_scales)
+        xt_w = load_words8("xt_w", xt_words)
+        xo_w = load_words8("xo_w", xo_words)
+        load_plane(w_s, w_scales)
+        l2 = load_list("l2", offs2)
+        load_plane(xo_s, xo_scales)
+        l3 = load_list("l3", offs3)
+        l4 = load_list("l4", offs4)
+        l5 = load_list("l5", offs5)
+        ws_w = load_words4("ws_w", ws_words)
+        sx_w = load_words8("sx_w", sx_words)
+        load_plane(ws_s, ws_scales)
+        load_plane(sx_s, sx_scales)
+        wb_w = load_words4("wb_w", wb_words)
+        load_plane(wb_s, wb_scales)
+        l6 = load_list("l6", offs6)
+        l7 = load_list("l7", offs7)
+
+        pw = [tile("pw%d" % t, C, F32) for t in range(2)]
+        pv = [tile("pv%d" % t, C, F32) for t in range(2)]
+        for t in range(2):
+            nc.vector.memset(pw[t][:], 0.0)
+            nc.vector.memset(pv[t][:], 0.0)
+
+        wp_w = tile("wp_w", 2 * R, U8)
+        wp_s = tile("wp_s", R, U8)
+        nc.vector.tensor_copy(
+            wp_w[:].bitcast(U16).rearrange("p (t m) -> p t m", t=PACK),
+            w_w[:].bitcast(U16).rearrange("p (m t) -> p t m", t=PACK),
+        )
+        nc.vector.tensor_copy(
+            wp_s[:].rearrange("p (t m) -> p t m", t=PACK),
+            w_s[:].rearrange("p (m t) -> p t m", t=PACK),
+        )
+
+        gt_w = tile("gt_w", J, U32)
+        gt_s = tile("gt_s", J, U8)
+        go_w = tile("go_w", J, U32)
+        go_s = tile("go_s", J, U8)
+        nc.vector.tensor_copy(gt_w[:], xt_w[:].indirect(l1[:]))
+        nc.vector.tensor_copy(gt_s[:], xt_s[:].indirect(l1[:]))
+        nc.vector.tensor_copy(go_w[:], xo_w[:].indirect(l2[:]))
+        nc.vector.tensor_copy(go_s[:], xo_s[:].indirect(l2[:]))
+
+        pw += [tile("pw2", C, F32, "w_w"), tile("pw3", C, F32, "xt_s")]
+        pv += [tile("pv2", C, F32, "xt_w"), tile("pv3", C, F32, "xo_w")]
+        for t in range(2, PACK):
+            nc.gpsimd.memset(pw[t][:], 0.0)
+            nc.gpsimd.memset(pv[t][:], 0.0)
+
+        def first_stage(name, words, scales, fmt):
+            banks = []
+            for h in range(2):
+                bank = ps.tile([P, 2, J], F32, name="%s%d" % (name, h))
+                for u in range(2):
+                    t = 2 * h + u
+                    nc.tensor.matmul_mx(
+                        out=bank[:, u, :],
+                        lhsT=wp_w[:, 2 * P * t : 2 * P * (t + 1)].bitcast(E2M1),
+                        lhsT_scale=wp_s[:, P * t : P * (t + 1)],
+                        rhs=words[:].bitcast(fmt),
+                        rhs_scale=scales[:],
+                        start=True,
+                        stop=True,
+                    )
+                banks.append(bank)
+            return banks
+
+        a_ps = first_stage("a_ps", gt_w, gt_s, E5M2)
+        b_ps = first_stage("b_ps", go_w, go_s, E4M3)
+
+        p_ps = [ps.tile([P, O], F32, name="p_ps%d" % h) for h in range(2)]
+        for h in range(2):
+            nc.tensor.matmul_mx(
+                out=p_ps[h][:],
+                lhsT=ws_w[:, 2 * P * h : 2 * P * (h + 1)].bitcast(E2M1),
+                lhsT_scale=ws_s[:, P * h : P * (h + 1)],
+                rhs=sx_w[:].bitcast(E4M3),
+                rhs_scale=sx_s[:],
+                start=True,
+                stop=False,
+            )
+
+        a_sb = [sb.tile([P, 2, J], F32, name="a_sb%d" % h) for h in range(2)]
+        b_sb = [sb.tile([P, 2, J], F32, name="b_sb%d" % h) for h in range(2)]
+        pg = [tile("pg%d" % t, C, F32) for t in range(PACK)]
+        hid = sb.tile([P, PACK, O], BF16, name="hid", align_bytes=64)
+        nc.scalar.copy(a_sb[0][:], a_ps[0][:])
+        nc.vector.tensor_copy(b_sb[0][:], b_ps[0][:])
+        for t in range(PACK):
+            h, u = divmod(t, 2)
+            if t == 2:
+                nc.scalar.copy(a_sb[1][:], a_ps[1][:])
+                nc.scalar.copy(b_sb[1][:], b_ps[1][:])
+            nc.scalar.activation(pw[t][:].indirect(l3[:]), a_sb[h][:, u, :], COPY)
+            nc.vector.tensor_copy(pv[t][:].indirect(l4[:]), b_sb[h][:, u, :])
+        for t in range(PACK - 1):
+            nc.gpsimd.tensor_tensor(pg[t][:], pw[t][:], pv[t][:], ADD)
+        nc.vector.tensor_copy(hid[:, 0, :], pg[0][:].indirect(l5[:]))
+        nc.vector.tensor_tensor(pg[3][:], pw[3][:], pv[3][:], ADD)
+        for t in (1, 2):
+            nc.scalar.activation(hid[:, t, :], pg[t][:].indirect(l5[:]), COPY)
+        nc.vector.tensor_copy(hid[:, 3, :], pg[3][:].indirect(l5[:]))
+
+        hid_i = sb.tile([P, O, PACK], BF16, name="hid_i", align_bytes=64)
+        nc.vector.tensor_copy(
+            hid_i[:].rearrange("p (c i) t -> p c t i", i=4),
+            hid[:].rearrange("p t (c i) -> p c t i", i=4),
+        )
+        hq_w = tile("hq_w", O, U32)
+        hq_s = tile("hq_s", O, U8)
+        nc.vector.quantize_mx(out=hq_w[:].bitcast(E4M3), scales=hq_s[:], in_=hid_i[:].rearrange("p o t -> p (o t)"))
+
+        for h in range(2):
+            nc.tensor.matmul_mx(
+                out=p_ps[h][:],
+                lhsT=wb_w[:, 2 * P * h : 2 * P * (h + 1)].bitcast(E2M1),
+                lhsT_scale=wb_s[:, P * h : P * (h + 1)],
+                rhs=hq_w[:].bitcast(E4M3),
+                rhs_scale=hq_s[:],
+                start=False,
+                stop=True,
+            )
+
+        p_sb = [tile("p_sb%d" % h, O, F32) for h in range(2)]
+        g6 = [tile("g6_%d" % h, E, F32) for h in range(2)]
+        g7 = [tile("g7_%d" % h, E, F32) for h in range(2)]
+        y = [tile("y%d" % h, E, F32) for h in range(2)]
+        nc.vector.tensor_copy(p_sb[0][:], p_ps[0][:])
+        nc.scalar.copy(p_sb[1][:], p_ps[1][:])
+        nc.vector.tensor_copy(g6[0][:], p_sb[0][:].indirect(l6[:]))
+        nc.vector.tensor_copy(g7[0][:], p_sb[0][:].indirect(l7[:]))
+        nc.scalar.activation(g6[1][:], p_sb[1][:].indirect(l6[:]), COPY)
+        nc.scalar.activation(g7[1][:], p_sb[1][:].indirect(l7[:]), COPY)
+        for h in range(2):
+            nc.vector.tensor_tensor(y[h][:], g6[h][:], g7[h][:], MAX)
+            nc.sync.dma_start(out[P * h : P * (h + 1), :], y[h][:])

@@ -49,18 +49,18 @@ def tile_list_oneforboth_shared_skip_bestoftwo_kernel(
             nc.sync.dma_start(t[:].bitcast(I32), src[0].bitcast(I32))
             return t
 
-        def plane(name, src):
+        def plane(name, src, eng=nc.vector):
             t = tile(name, src.shape[2], U8)
-            nc.vector.memset(t[:].bitcast(I32), 0)
+            eng.memset(t[:].bitcast(I32), 0)
             return t
 
-        def load_plane(t, src):
-            for q in range(4):
-                nc.sync.dma_start(t[32 * q : 32 * q + 4, :].bitcast(I32), src[0, 4 * q : 4 * q + 4, :].bitcast(I32))
+        def load_plane(t, src, quadrants=range(4), eng=nc.sync):
+            for q in quadrants:
+                eng.dma_start(t[32 * q : 32 * q + 4, :].bitcast(I32), src[0, 4 * q : 4 * q + 4, :].bitcast(I32))
 
         xt_s = plane("xt_s", xt_scales)
         w_s = plane("w_s", w_scales)
-        xo_s = plane("xo_s", xo_scales)
+        xo_s = plane("xo_s", xo_scales, nc.gpsimd)
         wb_s = plane("wb_s", wb_scales)
         ws_s = plane("ws_s", ws_scales)
         sx_s = plane("sx_s", sx_scales)
@@ -68,11 +68,13 @@ def tile_list_oneforboth_shared_skip_bestoftwo_kernel(
         l1 = load_list("l1", offs)
         w_w = load_words4("w_w", w_words)
         load_plane(xt_s, xt_scales)
+        load_plane(w_s, w_scales, (0,))
         xt_w = load_words8("xt_w", xt_words)
-        xo_w = load_words8("xo_w", xo_words)
-        load_plane(w_s, w_scales)
+        load_plane(w_s, w_scales, (1, 2, 3))
         l2 = load_list("l2", offs2)
-        load_plane(xo_s, xo_scales)
+        xo_w = load_words8("xo_w", xo_words)
+        load_plane(xo_s, xo_scales, (2, 3), nc.gpsimd)
+        load_plane(xo_s, xo_scales, (0, 1))
         l3 = load_list("l3", offs3)
         l4 = load_list("l4", offs4)
         l5 = load_list("l5", offs5)
@@ -97,10 +99,11 @@ def tile_list_oneforboth_shared_skip_bestoftwo_kernel(
             wp_w[:].bitcast(U16).rearrange("p (t m) -> p t m", t=PACK),
             w_w[:].bitcast(U16).rearrange("p (m t) -> p t m", t=PACK),
         )
-        nc.vector.tensor_copy(
-            wp_s[:].rearrange("p (t m) -> p t m", t=PACK),
-            w_s[:].rearrange("p (m t) -> p t m", t=PACK),
-        )
+        for ts in (slice(0, 1), slice(1, PACK)):
+            nc.vector.tensor_copy(
+                wp_s[:].rearrange("p (t m) -> p t m", t=PACK)[:, ts, :],
+                w_s[:].rearrange("p (m t) -> p t m", t=PACK)[:, ts, :],
+            )
 
         gt_w = tile("gt_w", J, U32)
         gt_s = tile("gt_s", J, U8)
@@ -111,18 +114,17 @@ def tile_list_oneforboth_shared_skip_bestoftwo_kernel(
         nc.vector.tensor_copy(go_w[:], xo_w[:].indirect(l2[:]))
         nc.vector.tensor_copy(go_s[:], xo_s[:].indirect(l2[:]))
 
-        pw += [tile("pw2", C, F32, "w_w"), tile("pw3", C, F32, "xt_s")]
         pv += [tile("pv2", C, F32, "xt_w"), tile("pv3", C, F32, "xo_w")]
         for t in range(2, PACK):
-            nc.gpsimd.memset(pw[t][:], 0.0)
             nc.gpsimd.memset(pv[t][:], 0.0)
+
+        groups = ((0,), (1,), (2, 3))
 
         def first_stage(name, words, scales, fmt):
             banks = []
-            for h in range(2):
-                bank = ps.tile([P, 2, J], F32, name="%s%d" % (name, h))
-                for u in range(2):
-                    t = 2 * h + u
+            for g in groups:
+                bank = ps.tile([P, len(g), J], F32, name="%s%d" % (name, g[0]))
+                for u, t in enumerate(g):
                     nc.tensor.matmul_mx(
                         out=bank[:, u, :],
                         lhsT=wp_w[:, 2 * P * t : 2 * P * (t + 1)].bitcast(E2M1),
@@ -138,6 +140,10 @@ def tile_list_oneforboth_shared_skip_bestoftwo_kernel(
         a_ps = first_stage("a_ps", gt_w, gt_s, E5M2)
         b_ps = first_stage("b_ps", go_w, go_s, E4M3)
 
+        pw += [tile("pw2", C, F32, "wp_w"), tile("pw3", C, F32, "wp_s")]
+        for t in range(2, PACK):
+            nc.gpsimd.memset(pw[t][:], 0.0)
+
         p_ps = [ps.tile([P, O], F32, name="p_ps%d" % h) for h in range(2)]
         for h in range(2):
             nc.tensor.matmul_mx(
@@ -150,57 +156,58 @@ def tile_list_oneforboth_shared_skip_bestoftwo_kernel(
                 stop=False,
             )
 
-        a_sb = [sb.tile([P, 2, J], F32, name="a_sb%d" % h) for h in range(2)]
-        b_sb = [sb.tile([P, 2, J], F32, name="b_sb%d" % h) for h in range(2)]
+        a_sb = [sb.tile([P, len(g), J], F32, name="a_sb%d" % g[0]) for g in groups]
+        b_sb = [sb.tile([P, len(g), J], F32, name="b_sb%d" % g[0]) for g in groups]
         pg = [tile("pg%d" % t, C, F32) for t in range(PACK)]
         hid = sb.tile([P, PACK, O], BF16, name="hid", align_bytes=64)
-        nc.scalar.copy(a_sb[0][:], a_ps[0][:])
-        nc.vector.tensor_copy(b_sb[0][:], b_ps[0][:])
         for t in range(PACK):
-            h, u = divmod(t, 2)
+            h, u = (t, 0) if t < 2 else (2, t - 2)
+            if t < 2:
+                nc.scalar.copy(a_sb[h][:], a_ps[h][:])
+                nc.vector.tensor_copy(b_sb[h][:], b_ps[h][:])
             if t == 2:
-                nc.scalar.copy(a_sb[1][:], a_ps[1][:])
-                nc.scalar.copy(b_sb[1][:], b_ps[1][:])
+                nc.scalar.copy(b_sb[2][:], b_ps[2][:])
+                nc.scalar.copy(a_sb[2][:], a_ps[2][:])
             nc.scalar.activation(pw[t][:].indirect(l3[:]), a_sb[h][:, u, :], COPY)
             nc.vector.tensor_copy(pv[t][:].indirect(l4[:]), b_sb[h][:, u, :])
         for t in range(PACK - 1):
             nc.gpsimd.tensor_tensor(pg[t][:], pw[t][:], pv[t][:], ADD)
-        nc.vector.tensor_copy(hid[:, 0, :], pg[0][:].indirect(l5[:]))
         nc.vector.tensor_tensor(pg[3][:], pw[3][:], pv[3][:], ADD)
-        for t in (1, 2):
+        for t in range(PACK - 1):
             nc.scalar.activation(hid[:, t, :], pg[t][:].indirect(l5[:]), COPY)
         nc.vector.tensor_copy(hid[:, 3, :], pg[3][:].indirect(l5[:]))
 
-        hid_i = sb.tile([P, O, PACK], BF16, name="hid_i", align_bytes=64)
-        nc.vector.tensor_copy(
-            hid_i[:].rearrange("p (c i) t -> p c t i", i=4),
-            hid[:].rearrange("p t (c i) -> p c t i", i=4),
-        )
-        hq_w = tile("hq_w", O, U32)
-        hq_s = tile("hq_s", O, U8)
-        nc.vector.quantize_mx(out=hq_w[:].bitcast(E4M3), scales=hq_s[:], in_=hid_i[:].rearrange("p o t -> p (o t)"))
-
-        for h in range(2):
-            nc.tensor.matmul_mx(
-                out=p_ps[h][:],
-                lhsT=wb_w[:, 2 * P * h : 2 * P * (h + 1)].bitcast(E2M1),
-                lhsT_scale=wb_s[:, P * h : P * (h + 1)],
-                rhs=hq_w[:].bitcast(E4M3),
-                rhs_scale=hq_s[:],
-                start=False,
-                stop=True,
+        HO = O // 2
+        hid_i = [sb.tile([P, HO, PACK], BF16, name="hid_i%d" % s, align_bytes=64) for s in range(2)]
+        hq_w = [tile("hq_w%d" % s, HO, U32) for s in range(2)]
+        hq_s = [tile("hq_s%d" % s, HO, U8) for s in range(2)]
+        for s, cp in enumerate((nc.vector.tensor_copy, nc.scalar.copy)):
+            cp(
+                hid_i[s][:].rearrange("p (c i) t -> p c t i", i=4),
+                hid[:, :, HO * s : HO * (s + 1)].rearrange("p t (c i) -> p c t i", i=4),
             )
+        for s in range(2):
+            nc.vector.quantize_mx(out=hq_w[s][:].bitcast(E4M3), scales=hq_s[s][:], in_=hid_i[s][:].rearrange("p o t -> p (o t)"))
+            for h in (1, 0):
+                nc.tensor.matmul_mx(
+                    out=p_ps[h][:, HO * s : HO * (s + 1)],
+                    lhsT=wb_w[:, 2 * P * h : 2 * P * (h + 1)].bitcast(E2M1),
+                    lhsT_scale=wb_s[:, P * h : P * (h + 1)],
+                    rhs=hq_w[s][:].bitcast(E4M3),
+                    rhs_scale=hq_s[s][:],
+                    start=False,
+                    stop=(s == 1),
+                )
 
         p_sb = [tile("p_sb%d" % h, O, F32) for h in range(2)]
-        g6 = [tile("g6_%d" % h, E, F32) for h in range(2)]
-        g7 = [tile("g7_%d" % h, E, F32) for h in range(2)]
-        y = [tile("y%d" % h, E, F32) for h in range(2)]
-        nc.vector.tensor_copy(p_sb[0][:], p_ps[0][:])
+        g6 = sb.tile([P, 2, E], F32, name="g6")
+        g7 = sb.tile([P, 2, E], F32, name="g7")
+        y = sb.tile([P, 2, E], F32, name="y")
         nc.scalar.copy(p_sb[1][:], p_ps[1][:])
-        nc.vector.tensor_copy(g6[0][:], p_sb[0][:].indirect(l6[:]))
-        nc.vector.tensor_copy(g7[0][:], p_sb[0][:].indirect(l7[:]))
-        nc.scalar.activation(g6[1][:], p_sb[1][:].indirect(l6[:]), COPY)
-        nc.scalar.activation(g7[1][:], p_sb[1][:].indirect(l7[:]), COPY)
-        for h in range(2):
-            nc.vector.tensor_tensor(y[h][:], g6[h][:], g7[h][:], MAX)
-            nc.sync.dma_start(out[P * h : P * (h + 1), :], y[h][:])
+        nc.vector.tensor_copy(p_sb[0][:], p_ps[0][:])
+        nc.scalar.activation(g6[:, 1, :], p_sb[1][:].indirect(l6[:]), COPY)
+        nc.scalar.activation(g7[:, 1, :], p_sb[1][:].indirect(l7[:]), COPY)
+        nc.vector.tensor_copy(g6[:, 0, :], p_sb[0][:].indirect(l6[:]))
+        nc.vector.tensor_copy(g7[:, 0, :], p_sb[0][:].indirect(l7[:]))
+        nc.vector.tensor_tensor(y[:], g6[:], g7[:], MAX)
+        nc.sync.dma_start(out.rearrange("(h p) e -> p h e", h=2), y[:])

@@ -61,9 +61,10 @@ def tile_list_oneforboth_shared_skip_bestoftwo_kernel(
         xt_s = plane("xt_s", xt_scales)
         w_s = plane("w_s", w_scales)
         xo_s = plane("xo_s", xo_scales, nc.gpsimd)
-        wb_s = plane("wb_s", wb_scales)
-        ws_s = plane("ws_s", ws_scales)
-        sx_s = plane("sx_s", sx_scales)
+        load_plane(xo_s, xo_scales, (2, 3), nc.gpsimd)
+        wb_s = plane("wb_s", wb_scales, nc.gpsimd)
+        ws_s = plane("ws_s", ws_scales, nc.gpsimd)
+        sx_s = plane("sx_s", sx_scales, nc.gpsimd)
 
         l1 = load_list("l1", offs)
         w_w = load_words4("w_w", w_words)
@@ -73,7 +74,6 @@ def tile_list_oneforboth_shared_skip_bestoftwo_kernel(
         load_plane(w_s, w_scales, (1, 2, 3))
         l2 = load_list("l2", offs2)
         xo_w = load_words8("xo_w", xo_words)
-        load_plane(xo_s, xo_scales, (2, 3), nc.gpsimd)
         load_plane(xo_s, xo_scales, (0, 1))
         l3 = load_list("l3", offs3)
         l4 = load_list("l4", offs4)
@@ -90,8 +90,8 @@ def tile_list_oneforboth_shared_skip_bestoftwo_kernel(
         pw = [tile("pw%d" % t, C, F32) for t in range(2)]
         pv = [tile("pv%d" % t, C, F32) for t in range(2)]
         for t in range(2):
-            nc.vector.memset(pw[t][:], 0.0)
-            nc.vector.memset(pv[t][:], 0.0)
+            nc.gpsimd.memset(pw[t][:], 0.0)
+            nc.gpsimd.memset(pv[t][:], 0.0)
 
         wp_w = tile("wp_w", 2 * R, U8)
         wp_s = tile("wp_s", R, U8)
@@ -114,7 +114,7 @@ def tile_list_oneforboth_shared_skip_bestoftwo_kernel(
         nc.vector.tensor_copy(go_w[:], xo_w[:].indirect(l2[:]))
         nc.vector.tensor_copy(go_s[:], xo_s[:].indirect(l2[:]))
 
-        pv += [tile("pv2", C, F32, "xt_w"), tile("pv3", C, F32, "xo_w")]
+        pv += [tile("pv2", C, F32, "xo_w"), tile("pv3", C, F32, "xo_s")]
         for t in range(2, PACK):
             nc.gpsimd.memset(pv[t][:], 0.0)
 
@@ -160,16 +160,20 @@ def tile_list_oneforboth_shared_skip_bestoftwo_kernel(
         b_sb = [sb.tile([P, len(g), J], F32, name="b_sb%d" % g[0]) for g in groups]
         pg = [tile("pg%d" % t, C, F32) for t in range(PACK)]
         hid = sb.tile([P, PACK, O], BF16, name="hid", align_bytes=64)
-        for t in range(PACK):
-            h, u = (t, 0) if t < 2 else (2, t - 2)
-            if t < 2:
-                nc.scalar.copy(a_sb[h][:], a_ps[h][:])
-                nc.vector.tensor_copy(b_sb[h][:], b_ps[h][:])
-            if t == 2:
-                nc.scalar.copy(b_sb[2][:], b_ps[2][:])
-                nc.scalar.copy(a_sb[2][:], a_ps[2][:])
-            nc.scalar.activation(pw[t][:].indirect(l3[:]), a_sb[h][:, u, :], COPY)
-            nc.vector.tensor_copy(pv[t][:].indirect(l4[:]), b_sb[h][:, u, :])
+
+        nc.scalar.copy(a_sb[0][:], a_ps[0][:])
+        nc.scalar.copy(a_sb[1][:], a_ps[1][:])
+        nc.scalar.activation(pw[0][:].indirect(l3[:]), a_sb[0][:, 0, :], COPY)
+        nc.vector.tensor_copy(pw[1][:].indirect(l3[:]), a_sb[1][:, 0, :])
+        nc.vector.tensor_copy(b_sb[0][:], b_ps[0][:])
+        nc.scalar.copy(b_sb[1][:], b_ps[1][:])
+        nc.vector.tensor_copy(pv[0][:].indirect(l4[:]), b_sb[0][:, 0, :])
+        nc.scalar.activation(pv[1][:].indirect(l4[:]), b_sb[1][:, 0, :], COPY)
+        nc.scalar.copy(a_sb[2][:], a_ps[2][:])
+        nc.vector.tensor_copy(b_sb[2][:], b_ps[2][:])
+        for u in range(2):
+            nc.scalar.activation(pw[2 + u][:].indirect(l3[:]), a_sb[2][:, u, :], COPY)
+            nc.vector.tensor_copy(pv[2 + u][:].indirect(l4[:]), b_sb[2][:, u, :])
         for t in range(PACK - 1):
             nc.gpsimd.tensor_tensor(pg[t][:], pw[t][:], pv[t][:], ADD)
         nc.vector.tensor_tensor(pg[3][:], pw[3][:], pv[3][:], ADD)

@@ -2,7 +2,7 @@ from contextlib import ExitStack
 
 import concourse.mybir as mybir
 
-K, T, Z, J, R, C, O, N, L, E = 512, 1024, 1024, 256, 512, 512, 256, 256, 512, 128
+K, J, R, C, O, N, L, E = 512, 256, 512, 512, 256, 256, 512, 128
 FLOPS = 2 * (2 * K * R * J + R * N * O + L * N * O)
 
 F32 = mybir.dt.float32
@@ -20,6 +20,9 @@ MAX = mybir.AluOpType.max
 
 P = 128
 PACK = 4
+QUADRANTS = 4
+O_HALF = O // 2
+BANK_SLICES = ((0,), (1,), (2, 3))
 
 
 def tile_list_oneforboth_shared_skip_bestoftwo_kernel(
@@ -28,190 +31,184 @@ def tile_list_oneforboth_shared_skip_bestoftwo_kernel(
 ):
     nc = tc.nc
     with ExitStack() as ctx:
-        sb = ctx.enter_context(tc.tile_pool(name="sb", bufs=1))
-        ps = ctx.enter_context(tc.psum_pool(name="ps", bufs=1))
+        sbuf = ctx.enter_context(tc.tile_pool(name="sbuf", bufs=1))
+        psum = ctx.enter_context(tc.psum_pool(name="psum", bufs=1))
 
-        def tile(name, cols, dtype, tag=None):
-            return sb.tile([P, cols], dtype, name=name, tag=tag or name, align_bytes=64)
+        def tile(name, shape, dtype, reuses=None):
+            return sbuf.tile([P] + shape, dtype, name=name, tag=reuses or name, align_bytes=64)
 
         def load_list(name, src):
-            t = sb.tile([P, src.shape[1]], U16, name=name)
-            nc.sync.dma_start(t[:], src)
-            return t
+            offsets = sbuf.tile([P, src.shape[1]], U16, name=name)
+            nc.sync.dma_start(offsets[:], src)
+            return offsets
 
-        def load_words8(name, src):
-            t = tile(name, src.shape[2], U32)
-            nc.sync.dma_start(t[:].bitcast(I32), src[0].rearrange("p n t -> p (n t)").bitcast(I32))
-            return t
+        def load_fp8_words(name, src):
+            words = tile(name, [src.shape[2]], U32)
+            nc.sync.dma_start(words[:].bitcast(I32), src[0].rearrange("p n t -> p (n t)").bitcast(I32))
+            return words
 
-        def load_words4(name, src):
-            t = tile(name, src.shape[2], U8)
-            nc.sync.dma_start(t[:].bitcast(I32), src[0].bitcast(I32))
-            return t
+        def load_fp4_words(name, src):
+            words = tile(name, [src.shape[2]], U8)
+            nc.sync.dma_start(words[:].bitcast(I32), src[0].bitcast(I32))
+            return words
 
-        def plane(name, src, eng=nc.vector):
-            t = tile(name, src.shape[2], U8)
-            eng.memset(t[:].bitcast(I32), 0)
-            return t
+        def cleared_scales(name, src):
+            scales = tile(name, [src.shape[2]], U8)
+            nc.vector.memset(scales[:].bitcast(I32), 0)
+            return scales
 
-        def load_plane(t, src, quadrants=range(4), eng=nc.sync):
+        def load_scales(scales, src, quadrants=range(QUADRANTS)):
             for q in quadrants:
-                eng.dma_start(t[32 * q : 32 * q + 4, :].bitcast(I32), src[0, 4 * q : 4 * q + 4, :].bitcast(I32))
+                nc.sync.dma_start(
+                    scales[32 * q : 32 * q + 4, :].bitcast(I32),
+                    src[0, 4 * q : 4 * q + 4, :].bitcast(I32),
+                )
 
-        xt_s = plane("xt_s", xt_scales)
-        w_s = plane("w_s", w_scales)
-        xo_s = plane("xo_s", xo_scales, nc.gpsimd)
-        load_plane(xo_s, xo_scales, (2, 3), nc.gpsimd)
-        wb_s = plane("wb_s", wb_scales, nc.gpsimd)
-        ws_s = plane("ws_s", ws_scales, nc.gpsimd)
-        sx_s = plane("sx_s", sx_scales, nc.gpsimd)
+        def fp4_matmul(acc, words, scales, block, rhs_words, rhs_scales, rhs_format, start, stop):
+            nc.tensor.matmul_mx(
+                out=acc,
+                lhsT=words[:, 2 * P * block : 2 * P * (block + 1)].bitcast(E2M1),
+                lhsT_scale=scales[:, P * block : P * (block + 1)],
+                rhs=rhs_words[:].bitcast(rhs_format),
+                rhs_scale=rhs_scales[:],
+                start=start,
+                stop=stop,
+            )
 
-        l1 = load_list("l1", offs)
-        w_w = load_words4("w_w", w_words)
-        load_plane(xt_s, xt_scales)
-        load_plane(w_s, w_scales, (0,))
-        xt_w = load_words8("xt_w", xt_words)
-        load_plane(w_s, w_scales, (1, 2, 3))
-        l2 = load_list("l2", offs2)
-        xo_w = load_words8("xo_w", xo_words)
-        load_plane(xo_s, xo_scales, (0, 1))
-        l3 = load_list("l3", offs3)
-        l4 = load_list("l4", offs4)
-        l5 = load_list("l5", offs5)
-        ws_w = load_words4("ws_w", ws_words)
-        sx_w = load_words8("sx_w", sx_words)
-        load_plane(ws_s, ws_scales)
-        load_plane(sx_s, sx_scales)
-        wb_w = load_words4("wb_w", wb_words)
-        load_plane(wb_s, wb_scales)
-        l6 = load_list("l6", offs6)
-        l7 = load_list("l7", offs7)
+        xt_s = cleared_scales("xt_s", xt_scales)
+        w_s = cleared_scales("w_s", w_scales)
+        xo_s = cleared_scales("xo_s", xo_scales)
+        wb_s = cleared_scales("wb_s", wb_scales)
+        ws_s = cleared_scales("ws_s", ws_scales)
+        sx_s = cleared_scales("sx_s", sx_scales)
 
-        pw = [tile("pw%d" % t, C, F32) for t in range(2)]
-        pv = [tile("pv%d" % t, C, F32) for t in range(2)]
-        for t in range(2):
-            nc.gpsimd.memset(pw[t][:], 0.0)
-            nc.gpsimd.memset(pv[t][:], 0.0)
+        idx = load_list("idx", offs)
+        w_w = load_fp4_words("w_w", w_words)
+        load_scales(xt_s, xt_scales)
+        load_scales(w_s, w_scales, range(1))
+        xt_w = load_fp8_words("xt_w", xt_words)
+        load_scales(w_s, w_scales, range(1, QUADRANTS))
+        xo_w = load_fp8_words("xo_w", xo_words)
+        idx2 = load_list("idx2", offs2)
+        idx3 = load_list("idx3", offs3)
+        load_scales(xo_s, xo_scales)
+        idx4 = load_list("idx4", offs4)
+        idx5 = load_list("idx5", offs5)
+        ws_w = load_fp4_words("ws_w", ws_words)
+        sx_w = load_fp8_words("sx_w", sx_words)
+        load_scales(ws_s, ws_scales)
+        load_scales(sx_s, sx_scales)
+        wb_w = load_fp4_words("wb_w", wb_words)
+        load_scales(wb_s, wb_scales)
+        idx6 = load_list("idx6", offs6)
+        idx7 = load_list("idx7", offs7)
 
-        wp_w = tile("wp_w", 2 * R, U8)
-        wp_s = tile("wp_s", R, U8)
+        pw = [tile("pw%d" % t, [C], F32) for t in (0, 1)]
+        pv = [tile("pv%d" % t, [C], F32) for t in (0, 1)]
+        for t in (0, 1):
+            nc.vector.memset(pw[t][:], 0.0)
+            nc.vector.memset(pv[t][:], 0.0)
+
+        wp_w = tile("wp_w", [2 * R], U8)
+        wp_s = tile("wp_s", [R], U8)
         nc.vector.tensor_copy(
             wp_w[:].bitcast(U16).rearrange("p (t m) -> p t m", t=PACK),
             w_w[:].bitcast(U16).rearrange("p (m t) -> p t m", t=PACK),
         )
-        for ts in (slice(0, 1), slice(1, PACK)):
+        for slices in (slice(0, 1), slice(1, PACK)):
             nc.vector.tensor_copy(
-                wp_s[:].rearrange("p (t m) -> p t m", t=PACK)[:, ts, :],
-                w_s[:].rearrange("p (m t) -> p t m", t=PACK)[:, ts, :],
+                wp_s[:].rearrange("p (t m) -> p t m", t=PACK)[:, slices, :],
+                w_s[:].rearrange("p (m t) -> p t m", t=PACK)[:, slices, :],
             )
 
-        gt_w = tile("gt_w", J, U32)
-        gt_s = tile("gt_s", J, U8)
-        go_w = tile("go_w", J, U32)
-        go_s = tile("go_s", J, U8)
-        nc.vector.tensor_copy(gt_w[:], xt_w[:].indirect(l1[:]))
-        nc.vector.tensor_copy(gt_s[:], xt_s[:].indirect(l1[:]))
-        nc.vector.tensor_copy(go_w[:], xo_w[:].indirect(l2[:]))
-        nc.vector.tensor_copy(go_s[:], xo_s[:].indirect(l2[:]))
+        xtg_w = tile("xtg_w", [J], U32)
+        xtg_s = tile("xtg_s", [J], U8)
+        xog_w = tile("xog_w", [J], U32)
+        xog_s = tile("xog_s", [J], U8)
+        nc.vector.tensor_copy(xtg_w[:], xt_w[:].indirect(idx[:]))
+        nc.vector.tensor_copy(xtg_s[:], xt_s[:].indirect(idx[:]))
+        nc.vector.tensor_copy(xog_w[:], xo_w[:].indirect(idx2[:]))
+        nc.vector.tensor_copy(xog_s[:], xo_s[:].indirect(idx2[:]))
 
-        pv += [tile("pv2", C, F32, "xo_w"), tile("pv3", C, F32, "xo_s")]
-        for t in range(2, PACK):
-            nc.gpsimd.memset(pv[t][:], 0.0)
-
-        groups = ((0,), (1,), (2, 3))
-
-        def first_stage(name, words, scales, fmt):
+        def first_stage(name, words, scales, rhs_format):
             banks = []
-            for g in groups:
-                bank = ps.tile([P, len(g), J], F32, name="%s%d" % (name, g[0]))
-                for u, t in enumerate(g):
-                    nc.tensor.matmul_mx(
-                        out=bank[:, u, :],
-                        lhsT=wp_w[:, 2 * P * t : 2 * P * (t + 1)].bitcast(E2M1),
-                        lhsT_scale=wp_s[:, P * t : P * (t + 1)],
-                        rhs=words[:].bitcast(fmt),
-                        rhs_scale=scales[:],
-                        start=True,
-                        stop=True,
-                    )
+            for slices in BANK_SLICES:
+                bank = psum.tile([P, len(slices), J], F32, name="%s%d" % (name, slices[0]))
+                for u, t in enumerate(slices):
+                    fp4_matmul(bank[:, u, :], wp_w, wp_s, t, words, scales, rhs_format, True, True)
                 banks.append(bank)
             return banks
 
-        a_ps = first_stage("a_ps", gt_w, gt_s, E5M2)
-        b_ps = first_stage("b_ps", go_w, go_s, E4M3)
+        a_ps = first_stage("a_ps", xtg_w, xtg_s, E5M2)
+        b_ps = first_stage("b_ps", xog_w, xog_s, E4M3)
 
-        pw += [tile("pw2", C, F32, "wp_w"), tile("pw3", C, F32, "wp_s")]
-        for t in range(2, PACK):
+        pw += [tile("pw2", [C], F32, "wp_w"), tile("pw3", [C], F32, "wp_s")]
+        for t in (2, 3):
             nc.gpsimd.memset(pw[t][:], 0.0)
 
-        p_ps = [ps.tile([P, O], F32, name="p_ps%d" % h) for h in range(2)]
+        p_ps = [psum.tile([P, O], F32, name="p_ps%d" % h) for h in range(2)]
         for h in range(2):
-            nc.tensor.matmul_mx(
-                out=p_ps[h][:],
-                lhsT=ws_w[:, 2 * P * h : 2 * P * (h + 1)].bitcast(E2M1),
-                lhsT_scale=ws_s[:, P * h : P * (h + 1)],
-                rhs=sx_w[:].bitcast(E4M3),
-                rhs_scale=sx_s[:],
-                start=True,
-                stop=False,
-            )
+            fp4_matmul(p_ps[h][:], ws_w, ws_s, h, sx_w, sx_s, E4M3, True, False)
 
-        a_sb = [sb.tile([P, len(g), J], F32, name="a_sb%d" % g[0]) for g in groups]
-        b_sb = [sb.tile([P, len(g), J], F32, name="b_sb%d" % g[0]) for g in groups]
-        pg = [tile("pg%d" % t, C, F32) for t in range(PACK)]
-        hid = sb.tile([P, PACK, O], BF16, name="hid", align_bytes=64)
+        a_sb = [tile("a_sb0", [1, J], F32), tile("a_sb1", [1, J], F32, "xo_s"), tile("a_sb2", [2, J], F32)]
+        b_sb = [tile("b_sb%d" % slices[0], [len(slices), J], F32) for slices in BANK_SLICES]
 
         nc.scalar.copy(a_sb[0][:], a_ps[0][:])
-        nc.scalar.copy(a_sb[1][:], a_ps[1][:])
-        nc.scalar.activation(pw[0][:].indirect(l3[:]), a_sb[0][:, 0, :], COPY)
-        nc.vector.tensor_copy(pw[1][:].indirect(l3[:]), a_sb[1][:, 0, :])
+        nc.scalar.activation(pw[0][:].indirect(idx3[:]), a_sb[0][:, 0, :], COPY)
+        nc.vector.tensor_copy(a_sb[1][:], a_ps[1][:])
+        nc.vector.tensor_copy(pw[1][:].indirect(idx3[:]), a_sb[1][:, 0, :])
         nc.vector.tensor_copy(b_sb[0][:], b_ps[0][:])
         nc.scalar.copy(b_sb[1][:], b_ps[1][:])
-        nc.vector.tensor_copy(pv[0][:].indirect(l4[:]), b_sb[0][:, 0, :])
-        nc.scalar.activation(pv[1][:].indirect(l4[:]), b_sb[1][:, 0, :], COPY)
-        nc.scalar.copy(a_sb[2][:], a_ps[2][:])
-        nc.vector.tensor_copy(b_sb[2][:], b_ps[2][:])
-        for u in range(2):
-            nc.scalar.activation(pw[2 + u][:].indirect(l3[:]), a_sb[2][:, u, :], COPY)
-            nc.vector.tensor_copy(pv[2 + u][:].indirect(l4[:]), b_sb[2][:, u, :])
-        for t in range(PACK - 1):
-            nc.gpsimd.tensor_tensor(pg[t][:], pw[t][:], pv[t][:], ADD)
-        nc.vector.tensor_tensor(pg[3][:], pw[3][:], pv[3][:], ADD)
-        for t in range(PACK - 1):
-            nc.scalar.activation(hid[:, t, :], pg[t][:].indirect(l5[:]), COPY)
-        nc.vector.tensor_copy(hid[:, 3, :], pg[3][:].indirect(l5[:]))
+        nc.scalar.copy(b_sb[2][:], b_ps[2][:])
+        nc.vector.tensor_copy(pv[0][:].indirect(idx4[:]), b_sb[0][:, 0, :])
+        nc.scalar.activation(pv[1][:].indirect(idx4[:]), b_sb[1][:, 0, :], COPY)
 
-        HO = O // 2
-        hid_i = [sb.tile([P, HO, PACK], BF16, name="hid_i%d" % s, align_bytes=64) for s in range(2)]
-        hq_w = [tile("hq_w%d" % s, HO, U32) for s in range(2)]
-        hq_s = [tile("hq_s%d" % s, HO, U8) for s in range(2)]
-        for s, cp in enumerate((nc.vector.tensor_copy, nc.scalar.copy)):
-            cp(
+        pv += [tile("pv2", [C], F32, "a_sb0"), tile("pv3", [C], F32, "xo_s")]
+        for t in (2, 3):
+            nc.gpsimd.memset(pv[t][:], 0.0)
+
+        nc.scalar.copy(a_sb[2][:], a_ps[2][:])
+        for u, t in enumerate(BANK_SLICES[2]):
+            nc.scalar.activation(pw[t][:].indirect(idx3[:]), a_sb[2][:, u, :], COPY)
+            nc.vector.tensor_copy(pv[t][:].indirect(idx4[:]), b_sb[2][:, u, :])
+
+        last = PACK - 1
+        pg = [tile("pg%d" % t, [C], F32) for t in range(PACK)]
+        hid = tile("hid", [PACK, O], BF16)
+        for t in range(last):
+            nc.gpsimd.tensor_tensor(pg[t][:], pw[t][:], pv[t][:], ADD)
+        nc.vector.tensor_tensor(pg[last][:], pw[last][:], pv[last][:], ADD)
+        for t in range(last):
+            nc.scalar.activation(hid[:, t, :], pg[t][:].indirect(idx5[:]), COPY)
+        nc.vector.tensor_copy(hid[:, last, :], pg[last][:].indirect(idx5[:]))
+
+        hid_i = [tile("hid_i%d" % s, [O_HALF, PACK], BF16) for s in range(2)]
+        hq_w = [tile("hq_w%d" % s, [O_HALF], U32) for s in range(2)]
+        hq_s = [tile("hq_s%d" % s, [O_HALF], U8) for s in range(2)]
+        for s, copy in enumerate((nc.vector.tensor_copy, nc.scalar.copy)):
+            copy(
                 hid_i[s][:].rearrange("p (c i) t -> p c t i", i=4),
-                hid[:, :, HO * s : HO * (s + 1)].rearrange("p t (c i) -> p c t i", i=4),
+                hid[:, :, O_HALF * s : O_HALF * (s + 1)].rearrange("p t (c i) -> p c t i", i=4),
             )
         for s in range(2):
-            nc.vector.quantize_mx(out=hq_w[s][:].bitcast(E4M3), scales=hq_s[s][:], in_=hid_i[s][:].rearrange("p o t -> p (o t)"))
+            nc.vector.quantize_mx(
+                out=hq_w[s][:].bitcast(E4M3),
+                scales=hq_s[s][:],
+                in_=hid_i[s][:].rearrange("p o t -> p (o t)"),
+            )
             for h in (1, 0):
-                nc.tensor.matmul_mx(
-                    out=p_ps[h][:, HO * s : HO * (s + 1)],
-                    lhsT=wb_w[:, 2 * P * h : 2 * P * (h + 1)].bitcast(E2M1),
-                    lhsT_scale=wb_s[:, P * h : P * (h + 1)],
-                    rhs=hq_w[s][:].bitcast(E4M3),
-                    rhs_scale=hq_s[s][:],
-                    start=False,
-                    stop=(s == 1),
-                )
+                acc = p_ps[h][:, O_HALF * s : O_HALF * (s + 1)]
+                fp4_matmul(acc, wb_w, wb_s, h, hq_w[s], hq_s[s], E4M3, False, s == 1)
 
-        p_sb = [tile("p_sb%d" % h, O, F32) for h in range(2)]
-        g6 = sb.tile([P, 2, E], F32, name="g6")
-        g7 = sb.tile([P, 2, E], F32, name="g7")
-        y = sb.tile([P, 2, E], F32, name="y")
+        p_sb = [tile("p_sb%d" % h, [O], F32) for h in range(2)]
+        p6 = tile("p6", [2, E], F32)
+        p7 = tile("p7", [2, E], F32)
+        y = tile("y", [2, E], F32)
         nc.scalar.copy(p_sb[1][:], p_ps[1][:])
         nc.vector.tensor_copy(p_sb[0][:], p_ps[0][:])
-        nc.scalar.activation(g6[:, 1, :], p_sb[1][:].indirect(l6[:]), COPY)
-        nc.scalar.activation(g7[:, 1, :], p_sb[1][:].indirect(l7[:]), COPY)
-        nc.vector.tensor_copy(g6[:, 0, :], p_sb[0][:].indirect(l6[:]))
-        nc.vector.tensor_copy(g7[:, 0, :], p_sb[0][:].indirect(l7[:]))
-        nc.vector.tensor_tensor(y[:], g6[:], g7[:], MAX)
+        nc.scalar.activation(p6[:, 1, :], p_sb[1][:].indirect(idx6[:]), COPY)
+        nc.scalar.activation(p7[:, 1, :], p_sb[1][:].indirect(idx7[:]), COPY)
+        nc.vector.tensor_copy(p6[:, 0, :], p_sb[0][:].indirect(idx6[:]))
+        nc.vector.tensor_copy(p7[:, 0, :], p_sb[0][:].indirect(idx7[:]))
+        nc.vector.tensor_tensor(y[:], p6[:], p7[:], MAX)
         nc.sync.dma_start(out.rearrange("(h p) e -> p h e", h=2), y[:])

from contextlib import ExitStack

import concourse.mybir as mybir

K, J, R, C, O, N, L, E = 512, 256, 512, 512, 256, 256, 512, 128
FLOPS = 2 * (2 * K * R * J + R * N * O + L * N * O)

F32 = mybir.dt.float32
BF16 = mybir.dt.bfloat16
I32 = mybir.dt.int32
U32 = mybir.dt.uint32
U16 = mybir.dt.uint16
U8 = mybir.dt.uint8
E4M3 = mybir.dt.float8_e4m3fn_x4
E5M2 = mybir.dt.float8_e5m2_x4
E2M1 = mybir.dt.float4_e2m1fn_x4
COPY = mybir.ActivationFunctionType.Copy
ADD = mybir.AluOpType.add
MAX = mybir.AluOpType.max

P = 128
PACK = 4
QUADRANTS = 4
O_HALF = O // 2
BANK_SLICES = ((0,), (1,), (2, 3))


def tile_list_oneforboth_shared_skip_bestoftwo_kernel(
    tc, xt_words, xt_scales, xo_words, xo_scales, w_words, w_scales, wb_words, wb_scales,
    sx_words, sx_scales, ws_words, ws_scales, offs, offs2, offs3, offs4, offs5, offs6, offs7, out,
):
    nc = tc.nc
    with ExitStack() as ctx:
        sbuf = ctx.enter_context(tc.tile_pool(name="sbuf", bufs=1))
        psum = ctx.enter_context(tc.psum_pool(name="psum", bufs=1))

        def tile(name, shape, dtype, reuses=None):
            return sbuf.tile([P] + shape, dtype, name=name, tag=reuses or name, align_bytes=64)

        def load_list(name, src):
            offsets = sbuf.tile([P, src.shape[1]], U16, name=name)
            nc.sync.dma_start(offsets[:], src)
            return offsets

        def load_fp8_words(name, src):
            words = tile(name, [src.shape[2]], U32)
            nc.sync.dma_start(words[:].bitcast(I32), src[0].rearrange("p n t -> p (n t)").bitcast(I32))
            return words

        def load_fp4_words(name, src):
            words = tile(name, [src.shape[2]], U8)
            nc.sync.dma_start(words[:].bitcast(I32), src[0].bitcast(I32))
            return words

        def cleared_scales(name, src):
            scales = tile(name, [src.shape[2]], U8)
            nc.vector.memset(scales[:].bitcast(I32), 0)
            return scales

        def load_scales(scales, src, quadrants=range(QUADRANTS)):
            for q in quadrants:
                nc.sync.dma_start(
                    scales[32 * q : 32 * q + 4, :].bitcast(I32),
                    src[0, 4 * q : 4 * q + 4, :].bitcast(I32),
                )

        def fp4_matmul(acc, words, scales, block, rhs_words, rhs_scales, rhs_format, start, stop):
            nc.tensor.matmul_mx(
                out=acc,
                lhsT=words[:, 2 * P * block : 2 * P * (block + 1)].bitcast(E2M1),
                lhsT_scale=scales[:, P * block : P * (block + 1)],
                rhs=rhs_words[:].bitcast(rhs_format),
                rhs_scale=rhs_scales[:],
                start=start,
                stop=stop,
            )

        xt_s = cleared_scales("xt_s", xt_scales)
        w_s = cleared_scales("w_s", w_scales)
        xo_s = cleared_scales("xo_s", xo_scales)
        wb_s = cleared_scales("wb_s", wb_scales)
        ws_s = cleared_scales("ws_s", ws_scales)
        sx_s = cleared_scales("sx_s", sx_scales)

        idx = load_list("idx", offs)
        w_w = load_fp4_words("w_w", w_words)
        load_scales(xt_s, xt_scales)
        load_scales(w_s, w_scales, range(1))
        xt_w = load_fp8_words("xt_w", xt_words)
        load_scales(w_s, w_scales, range(1, QUADRANTS))
        xo_w = load_fp8_words("xo_w", xo_words)
        idx2 = load_list("idx2", offs2)
        idx3 = load_list("idx3", offs3)
        load_scales(xo_s, xo_scales)
        idx4 = load_list("idx4", offs4)
        idx5 = load_list("idx5", offs5)
        ws_w = load_fp4_words("ws_w", ws_words)
        sx_w = load_fp8_words("sx_w", sx_words)
        load_scales(ws_s, ws_scales)
        load_scales(sx_s, sx_scales)
        wb_w = load_fp4_words("wb_w", wb_words)
        load_scales(wb_s, wb_scales)
        idx6 = load_list("idx6", offs6)
        idx7 = load_list("idx7", offs7)

        pw = [tile("pw%d" % t, [C], F32) for t in (0, 1)]
        pv = [tile("pv%d" % t, [C], F32) for t in (0, 1)]
        for t in (0, 1):
            nc.vector.memset(pw[t][:], 0.0)
            nc.vector.memset(pv[t][:], 0.0)

        wp_w = tile("wp_w", [2 * R], U8)
        wp_s = tile("wp_s", [R], U8)
        nc.vector.tensor_copy(
            wp_w[:].bitcast(U16).rearrange("p (t m) -> p t m", t=PACK),
            w_w[:].bitcast(U16).rearrange("p (m t) -> p t m", t=PACK),
        )
        for slices in (slice(0, 1), slice(1, PACK)):
            nc.vector.tensor_copy(
                wp_s[:].rearrange("p (t m) -> p t m", t=PACK)[:, slices, :],
                w_s[:].rearrange("p (m t) -> p t m", t=PACK)[:, slices, :],
            )

        xtg_w = tile("xtg_w", [J], U32)
        xtg_s = tile("xtg_s", [J], U8)
        xog_w = tile("xog_w", [J], U32)
        xog_s = tile("xog_s", [J], U8)
        nc.vector.tensor_copy(xtg_w[:], xt_w[:].indirect(idx[:]))
        nc.vector.tensor_copy(xtg_s[:], xt_s[:].indirect(idx[:]))
        nc.vector.tensor_copy(xog_w[:], xo_w[:].indirect(idx2[:]))
        nc.vector.tensor_copy(xog_s[:], xo_s[:].indirect(idx2[:]))

        def first_stage(name, words, scales, rhs_format):
            banks = []
            for slices in BANK_SLICES:
                bank = psum.tile([P, len(slices), J], F32, name="%s%d" % (name, slices[0]))
                for u, t in enumerate(slices):
                    fp4_matmul(bank[:, u, :], wp_w, wp_s, t, words, scales, rhs_format, True, True)
                banks.append(bank)
            return banks

        a_ps = first_stage("a_ps", xtg_w, xtg_s, E5M2)
        b_ps = first_stage("b_ps", xog_w, xog_s, E4M3)

        pw += [tile("pw2", [C], F32, "wp_w"), tile("pw3", [C], F32, "wp_s")]
        for t in (2, 3):
            nc.gpsimd.memset(pw[t][:], 0.0)

        p_ps = [psum.tile([P, O], F32, name="p_ps%d" % h) for h in range(2)]
        for h in range(2):
            fp4_matmul(p_ps[h][:], ws_w, ws_s, h, sx_w, sx_s, E4M3, True, False)

        a_sb = [tile("a_sb0", [1, J], F32), tile("a_sb1", [1, J], F32, "xo_s"), tile("a_sb2", [2, J], F32)]
        b_sb = [tile("b_sb%d" % slices[0], [len(slices), J], F32) for slices in BANK_SLICES]

        nc.scalar.copy(a_sb[0][:], a_ps[0][:])
        nc.scalar.activation(pw[0][:].indirect(idx3[:]), a_sb[0][:, 0, :], COPY)
        nc.vector.tensor_copy(a_sb[1][:], a_ps[1][:])
        nc.vector.tensor_copy(pw[1][:].indirect(idx3[:]), a_sb[1][:, 0, :])
        nc.vector.tensor_copy(b_sb[0][:], b_ps[0][:])
        nc.scalar.copy(b_sb[1][:], b_ps[1][:])
        nc.scalar.copy(b_sb[2][:], b_ps[2][:])
        nc.vector.tensor_copy(pv[0][:].indirect(idx4[:]), b_sb[0][:, 0, :])
        nc.scalar.activation(pv[1][:].indirect(idx4[:]), b_sb[1][:, 0, :], COPY)

        pv += [tile("pv2", [C], F32, "a_sb0"), tile("pv3", [C], F32, "xo_s")]
        for t in (2, 3):
            nc.gpsimd.memset(pv[t][:], 0.0)

        nc.scalar.copy(a_sb[2][:], a_ps[2][:])
        for u, t in enumerate(BANK_SLICES[2]):
            nc.scalar.activation(pw[t][:].indirect(idx3[:]), a_sb[2][:, u, :], COPY)
            nc.vector.tensor_copy(pv[t][:].indirect(idx4[:]), b_sb[2][:, u, :])

        last = PACK - 1
        pg = [tile("pg%d" % t, [C], F32) for t in range(PACK)]
        hid = tile("hid", [PACK, O], BF16)
        for t in range(last):
            nc.gpsimd.tensor_tensor(pg[t][:], pw[t][:], pv[t][:], ADD)
        nc.vector.tensor_tensor(pg[last][:], pw[last][:], pv[last][:], ADD)
        for t in range(last):
            nc.scalar.activation(hid[:, t, :], pg[t][:].indirect(idx5[:]), COPY)
        nc.vector.tensor_copy(hid[:, last, :], pg[last][:].indirect(idx5[:]))

        hid_i = [tile("hid_i%d" % s, [O_HALF, PACK], BF16) for s in range(2)]
        hq_w = [tile("hq_w%d" % s, [O_HALF], U32) for s in range(2)]
        hq_s = [tile("hq_s%d" % s, [O_HALF], U8) for s in range(2)]
        for s, copy in enumerate((nc.vector.tensor_copy, nc.scalar.copy)):
            copy(
                hid_i[s][:].rearrange("p (c i) t -> p c t i", i=4),
                hid[:, :, O_HALF * s : O_HALF * (s + 1)].rearrange("p t (c i) -> p c t i", i=4),
            )
        for s in range(2):
            nc.vector.quantize_mx(
                out=hq_w[s][:].bitcast(E4M3),
                scales=hq_s[s][:],
                in_=hid_i[s][:].rearrange("p o t -> p (o t)"),
            )
            for h in (1, 0):
                acc = p_ps[h][:, O_HALF * s : O_HALF * (s + 1)]
                fp4_matmul(acc, wb_w, wb_s, h, hq_w[s], hq_s[s], E4M3, False, s == 1)

        p_sb = [tile("p_sb%d" % h, [O], F32) for h in range(2)]
        p6 = tile("p6", [2, E], F32)
        p7 = tile("p7", [2, E], F32)
        y = tile("y", [2, E], F32)
        nc.scalar.copy(p_sb[1][:], p_ps[1][:])
        nc.vector.tensor_copy(p_sb[0][:], p_ps[0][:])
        nc.scalar.activation(p6[:, 1, :], p_sb[1][:].indirect(idx6[:]), COPY)
        nc.scalar.activation(p7[:, 1, :], p_sb[1][:].indirect(idx7[:]), COPY)
        nc.vector.tensor_copy(p6[:, 0, :], p_sb[0][:].indirect(idx6[:]))
        nc.vector.tensor_copy(p7[:, 0, :], p_sb[0][:].indirect(idx7[:]))
        nc.vector.tensor_tensor(y[:], p6[:], p7[:], MAX)
        nc.sync.dma_start(out.rearrange("(h p) e -> p h e", h=2), y[:])
